import numpy as np
CORES = [2,6,10,14]
N = 4
ROOT = 3
def setup_inputs(rng):
    return {"x": rng.standard_normal((N, 128, 128), dtype=np.float32)}
def reference(x):
    y = np.full(x.shape, np.nan, x.dtype)
    y[ROOT] = x.min(axis=0)
    return {"y": y}

@@ -1,0 +1,73 @@
+from concourse.bass import DstId, RemoteDMATransfer
+
+K = 4
+W = 128 * 128 // (128 * K)
+FOLD = [10, 12, 13, 15]
+
+SCRATCH = {
+    "src": ("dram", [K, 128, W], "float32"),
+    "inb": ("dram", [4, 128, W], "float32"),
+    "land": ("dram", [K, 128, W], "float32"),
+}
+SEMAPHORES = ["loaded", "sent", "arrived", "result", "stored"]
+
+
+def engines_of(src_core, topo, root):
+    n = 16 if topo.chip(src_core) == topo.chip(root) else 8
+    return n // K
+
+
+def rank_program(g, core, T, topo):
+    rank = T.rank_of(core)
+    root = T.cores[3]
+    is_fold = core in FOLD
+    if rank is None and not is_fold:
+        return
+
+    def dst_id(c):
+        rid, pid, _se = topo.addr(c)
+        return DstId(rid=rid, pnc=pid)
+
+    if rank is not None:
+        g.sync.dma_start(T.src[:], T.x[:]).then_inc(T.sem.loaded, 16)
+        g.wait_ge(T.sem.loaded, 16)
+
+        e = engines_of(core, topo, root)
+        transfers = []
+        for j in range(K):
+            if FOLD[j] == core:
+                continue
+            transfers.append(RemoteDMATransfer(
+                dst_ids=[dst_id(FOLD[j])],
+                dma_engine_mask=((1 << e) - 1) << (e * j),
+                remote_sem=T.sem.arrived,
+                src=T.src[j], dst=T.inb[rank]))
+        g.remote_dma_fused(transfers, local_sem=T.sem.sent)
+        sent = e * len(transfers)
+    else:
+        sent = 0
+
+    if is_fold:
+        j = FOLD.index(core)
+        need = 0
+        srcs = []
+        for r, c in enumerate(T.cores):
+            if c == core:
+                srcs.append(T.src[j])
+            else:
+                srcs.append(T.inb[r])
+                need += engines_of(c, topo, root)
+        g.wait_ge(T.sem.arrived, need)
+        g.remote_dma_fused([RemoteDMATransfer(
+            dst_ids=[dst_id(root)],
+            dma_engine_mask=0xFFFF,
+            remote_sem=T.sem.result,
+            srcs=srcs, dsts=[T.land[j]], alu_op=3)], local_sem=T.sem.sent)
+        sent += 16
+
+    if core == root:
+        g.sync.wait_ge(T.sem.result, 16 * K)
+        g.sync.dma_start(T.y[:], T.land[:]).then_inc(T.sem.stored, 16)
+        g.sync.wait_ge(T.sem.stored, 16)
+
+    g.wait_ge(T.sem.sent, sent)

@@ -1,20 +1,23 @@
 from concourse.bass import DstId, RemoteDMATransfer
 
 K = 4
-W = 128 * 128 // (128 * K)
-FOLD = [10, 12, 13, 15]
+C = 2
+P = K // C
+W = 128 // K
+FOLD = [12, 13, 10, 15]
 
 SCRATCH = {
     "src": ("dram", [K, 128, W], "float32"),
     "inb": ("dram", [4, 128, W], "float32"),
     "land": ("dram", [K, 128, W], "float32"),
 }
-SEMAPHORES = ["loaded", "sent", "arrived", "result", "stored"]
+SEMAPHORES = (["sent", "arrived"] + ["loaded%d" % c for c in range(C)] + ["result%d" % c for c in range(C)]
+              + ["stored%d" % c for c in range(C)])
 
 
 def engines_of(src_core, topo, root):
     n = 16 if topo.chip(src_core) == topo.chip(root) else 8
-    return n // K
+    return n // P
 
 
 def rank_program(g, core, T, topo):
@@ -23,29 +26,33 @@ def rank_program(g, core, T, topo):
     is_fold = core in FOLD
     if rank is None and not is_fold:
         return
+    queues = [g.sync, g.scalar]
 
     def dst_id(c):
         rid, pid, _se = topo.addr(c)
         return DstId(rid=rid, pnc=pid)
 
+    sent = 0
     if rank is not None:
-        g.sync.dma_start(T.src[:], T.x[:]).then_inc(T.sem.loaded, 16)
-        g.wait_ge(T.sem.loaded, 16)
-
+        for c in range(C):
+            queues[c % 2].dma_start(T.src[c * P:(c + 1) * P], T.x[c * P * W:(c + 1) * P * W, :]).then_inc(
+                T.sem["loaded%d" % c], 16)
         e = engines_of(core, topo, root)
-        transfers = []
-        for j in range(K):
-            if FOLD[j] == core:
-                continue
-            transfers.append(RemoteDMATransfer(
-                dst_ids=[dst_id(FOLD[j])],
-                dma_engine_mask=((1 << e) - 1) << (e * j),
-                remote_sem=T.sem.arrived,
-                src=T.src[j], dst=T.inb[rank]))
-        g.remote_dma_fused(transfers, local_sem=T.sem.sent)
-        sent = e * len(transfers)
-    else:
-        sent = 0
+        for c in range(C):
+            g.wait_ge(T.sem["loaded%d" % c], 16)
+            transfers = []
+            for p in range(P):
+                j = c * P + p
+                if FOLD[j] == core:
+                    continue
+                transfers.append(RemoteDMATransfer(
+                    dst_ids=[dst_id(FOLD[j])],
+                    dma_engine_mask=((1 << e) - 1) << (e * p),
+                    remote_sem=T.sem.arrived,
+                    src=T.src[j], dst=T.inb[rank]))
+            if transfers:
+                g.remote_dma_fused(transfers, local_sem=T.sem.sent)
+                sent += e * len(transfers)
 
     if is_fold:
         j = FOLD.index(core)
@@ -61,13 +68,17 @@ def rank_program(g, core, T, topo):
         g.remote_dma_fused([RemoteDMATransfer(
             dst_ids=[dst_id(root)],
             dma_engine_mask=0xFFFF,
-            remote_sem=T.sem.result,
+            remote_sem=T.sem["result%d" % (j // P)],
             srcs=srcs, dsts=[T.land[j]], alu_op=3)], local_sem=T.sem.sent)
         sent += 16
 
     if core == root:
-        g.sync.wait_ge(T.sem.result, 16 * K)
-        g.sync.dma_start(T.y[:], T.land[:]).then_inc(T.sem.stored, 16)
-        g.sync.wait_ge(T.sem.stored, 16)
+        for c in range(C):
+            q = queues[c % 2]
+            q.wait_ge(T.sem["result%d" % c], 16 * P)
+            q.dma_start(T.y[c * P * W:(c + 1) * P * W, :], T.land[c * P:(c + 1) * P]).then_inc(
+                T.sem["stored%d" % c], 16)
+        for c in range(C):
+            queues[c % 2].wait_ge(T.sem["stored%d" % c], 16)
 
     g.wait_ge(T.sem.sent, sent)

from concourse.bass import DstId, RemoteDMATransfer

K = 4
C = 2
P = K // C
W = 128 // K
FOLD = [12, 13, 10, 15]

SCRATCH = {
    "src": ("dram", [K, 128, W], "float32"),
    "inb": ("dram", [4, 128, W], "float32"),
    "land": ("dram", [K, 128, W], "float32"),
}
SEMAPHORES = (["sent", "arrived"] + ["loaded%d" % c for c in range(C)] + ["result%d" % c for c in range(C)]
              + ["stored%d" % c for c in range(C)])


def engines_of(src_core, topo, root):
    n = 16 if topo.chip(src_core) == topo.chip(root) else 8
    return n // P


def rank_program(g, core, T, topo):
    rank = T.rank_of(core)
    root = T.cores[3]
    is_fold = core in FOLD
    if rank is None and not is_fold:
        return
    queues = [g.sync, g.scalar]

    def dst_id(c):
        rid, pid, _se = topo.addr(c)
        return DstId(rid=rid, pnc=pid)

    sent = 0
    if rank is not None:
        for c in range(C):
            queues[c % 2].dma_start(T.src[c * P:(c + 1) * P], T.x[c * P * W:(c + 1) * P * W, :]).then_inc(
                T.sem["loaded%d" % c], 16)
        e = engines_of(core, topo, root)
        for c in range(C):
            g.wait_ge(T.sem["loaded%d" % c], 16)
            transfers = []
            for p in range(P):
                j = c * P + p
                if FOLD[j] == core:
                    continue
                transfers.append(RemoteDMATransfer(
                    dst_ids=[dst_id(FOLD[j])],
                    dma_engine_mask=((1 << e) - 1) << (e * p),
                    remote_sem=T.sem.arrived,
                    src=T.src[j], dst=T.inb[rank]))
            if transfers:
                g.remote_dma_fused(transfers, local_sem=T.sem.sent)
                sent += e * len(transfers)

    if is_fold:
        j = FOLD.index(core)
        need = 0
        srcs = []
        for r, c in enumerate(T.cores):
            if c == core:
                srcs.append(T.src[j])
            else:
                srcs.append(T.inb[r])
                need += engines_of(c, topo, root)
        g.wait_ge(T.sem.arrived, need)
        g.remote_dma_fused([RemoteDMATransfer(
            dst_ids=[dst_id(root)],
            dma_engine_mask=0xFFFF,
            remote_sem=T.sem["result%d" % (j // P)],
            srcs=srcs, dsts=[T.land[j]], alu_op=3)], local_sem=T.sem.sent)
        sent += 16

    if core == root:
        for c in range(C):
            q = queues[c % 2]
            q.wait_ge(T.sem["result%d" % c], 16 * P)
            q.dma_start(T.y[c * P * W:(c + 1) * P * W, :], T.land[c * P:(c + 1) * P]).then_inc(
                T.sem["stored%d" % c], 16)
        for c in range(C):
            queues[c % 2].wait_ge(T.sem["stored%d" % c], 16)

    g.wait_ge(T.sem.sent, sent)
